import numpy as np
import ml_dtypes


def mxq(x, axis, fmt="e4m3"):
    dtype, down = {"e4m3": (ml_dtypes.float8_e4m3fn, 7), "e5m2": (ml_dtypes.float8_e5m2, 14)}[fmt]
    v = np.moveaxis(np.asarray(x, np.float32).astype(ml_dtypes.bfloat16).astype(np.float64), axis, -1)
    blocks = v.reshape(v.shape[:-1] + (-1, 32))
    amax = np.abs(blocks).max(-1, keepdims=True)
    byte = np.maximum(np.where(amax > 0, np.frexp(amax)[1] - 1 + 127, 0) - down, 1)
    scale = np.exp2(byte - 127.0)
    codes = (blocks / scale).astype(np.float32).astype(dtype).astype(np.float64)
    return np.moveaxis((codes * scale).reshape(v.shape), -1, axis)


WIDE = False


def mx_kscale(k):
    if not WIDE:
        return np.ones(k)
    levels = np.array([10, -10, 5, -5, 0])
    if k % 512:
        return np.exp2(np.random.permutation(np.resize(levels, k // 32))).repeat(32)
    a = np.empty((k // 512, 16))
    for p in range(k // 512):
        a[p, :8] = np.random.permutation(np.resize(levels, 8))
        for g in range(8):
            far = levels[np.abs(levels - a[p, g]) >= 10]
            a[p, g + 8] = far[np.random.randint(len(far))]
    return np.exp2(a.ravel()).repeat(32)


def f64(x):
    return np.asarray(x).astype(np.float64)


def striped(idx):
    return np.tile(idx.reshape(-1, 16).T, (8, 1)).astype(np.uint16)


def unstriped(offs):
    return offs[:16].T.reshape(-1).astype(np.int64)


def striped8(idx):
    return np.concatenate([x.reshape(-1, 16).T for x in idx]).astype(np.uint16)


def runs(offs, k):
    lists = np.stack([offs[16 * r : 16 * r + 16].T.reshape(-1) for r in range(8)]).astype(np.int64)
    return lists[np.arange(k) % 512 // 64]


def pack_weight(w):
    k, n = w.shape
    w = f64(np.asarray(w, np.float32).astype(ml_dtypes.bfloat16)).reshape(k // 32, 32, n)
    amax = np.abs(w).max(1)
    byte = np.clip(np.where(amax > 0, np.frexp(amax)[1] - 1 + 127 - 7, 1), 1, 254)
    scaled = (w * np.exp2(127.0 - byte)[:, None, :]).reshape(k, n).astype(np.float32)
    words = np.ascontiguousarray(scaled.reshape(k // 512, 128, 4, n).transpose(0, 1, 3, 2)).astype(ml_dtypes.float8_e4m3fn).view(np.uint8)
    return words, np.ascontiguousarray(byte.astype(np.uint8).reshape(k // 512, 16, n))


def unpack_weight(words, scales):
    g, p, n, _ = words.shape
    vals = np.ascontiguousarray(words).view(ml_dtypes.float8_e4m3fn).astype(np.float64) * np.repeat(np.exp2(scales.astype(np.float64) - 127.0), 8, axis=1)[..., None]
    return vals.transpose(0, 1, 3, 2).reshape(g * 512, n)


E2M1 = np.array([0.0, 0.5, 1.0, 1.5, 2.0, 3.0, 4.0, 6.0, -0.0, -0.5, -1.0, -1.5, -2.0, -3.0, -4.0, -6.0])


def pack_fp4(w):
    k, n = w.shape
    w = f64(np.asarray(w, np.float32).astype(ml_dtypes.bfloat16)).reshape(k // 32, 32, n)
    amax = np.abs(w).max(1)
    mant, ex = np.frexp(amax / 6.0)
    byte = np.clip(np.where(amax > 0, np.where(mant > 0.5, ex, ex - 1) + 127, 1), 1, 254)
    scaled = (w * np.exp2(127.0 - byte)[:, None, :]).reshape(k, n).astype(np.float32)
    c = np.ascontiguousarray(scaled.reshape(k // 512, 128, 4, n).transpose(0, 1, 3, 2)).astype(ml_dtypes.float4_e2m1fn).view(np.uint8) & 0xF
    words = (c[..., 0::2] | (c[..., 1::2] << 4)).reshape(k // 512, 128, 2 * n)
    return np.ascontiguousarray(words), np.ascontiguousarray(byte.astype(np.uint8).reshape(k // 512, 16, n))


def unpack_fp4(words, scales):
    g, _, n = scales.shape
    words = np.ascontiguousarray(words).reshape(g, 128, n, 2)
    nib = np.empty((g, 128, n, 4), np.uint8)
    nib[..., 0::2] = words & 0xF
    nib[..., 1::2] = words >> 4
    vals = E2M1[nib] * np.repeat(np.exp2(scales.astype(np.float64) - 127.0), 8, axis=1)[..., None]
    return vals.transpose(0, 1, 3, 2).reshape(g * 512, n)


def sigmoid(v):
    return 1.0 / (1.0 + np.exp(-np.maximum(v, -700.0)))

def planes(y):
    n, m = y.shape
    v = y.astype(np.float32).astype(ml_dtypes.bfloat16).astype(np.float64).reshape(n // 32, 32, m)
    top = np.abs(v).max(1)
    byte = np.clip(np.where(top > 0, np.frexp(top)[1] - 1 + 127 - 7, 1), 1, 254)
    codes = (v * np.exp2(127.0 - byte)[:, None, :]).reshape(n, m).astype(np.float32).astype(ml_dtypes.float8_e4m3fn).view(np.uint8)
    words = codes.reshape(n // 512, 128, 4, m).transpose(0, 1, 3, 2)
    return np.ascontiguousarray(words), np.ascontiguousarray(byte.astype(np.uint8).reshape(n // 512, 16, m))


K, T, S, N, H = 512, 2048, 512, 512, 512


def setup_inputs():
    n = np.random.standard_normal
    s = mx_kscale(K)[:, None]
    u = mx_kscale(H)
    packed_xT = pack_weight(n((K, T)) * s)
    packed_w1 = pack_fp4(n((K, H)) / np.sqrt(K) / s)
    packed_w2 = pack_fp4(n((K, H)) / np.sqrt(K) / s)
    packed_w3 = pack_fp4(n((H, N)) / np.sqrt(H) / u[:, None])
    return {
        "x_words": packed_xT[0],
        "x_scales": packed_xT[1],
        "w1_words": packed_w1[0],
        "w1_scales": packed_w1[1],
        "w2_words": packed_w2[0],
        "w2_scales": packed_w2[1],
        "gn": (np.random.uniform(0.5, 1.5, (H, 1)) * u[:, None]).astype(np.float32),
        "w3_words": packed_w3[0],
        "w3_scales": packed_w3[1],
        "offs": striped(np.random.permutation(T)[:S]),
        "two": striped(np.random.permutation(T)[:S]),
        "n1": striped8(np.stack([np.random.permutation(S) for _ in range(8)])),
        "n2": striped8(np.stack([np.random.permutation(S) for _ in range(8)])),
        "n3": striped8(np.stack([np.random.permutation(S) for _ in range(8)])),
        "n4": striped8(np.stack([np.random.permutation(S) for _ in range(8)])),
        "n5": striped8(np.stack([np.random.permutation(S) for _ in range(8)])),
    }


def reference(x_words, x_scales, w1_words, w1_scales, w2_words, w2_scales, gn, w3_words, w3_scales, offs, two, n1, n2, n3, n4, n5):
    x_two = unpack_weight(x_words, x_scales)[:, unstriped(two)]
    d = unpack_fp4(w2_words, w2_scales).T @ x_two
    xq = unpack_weight(x_words, x_scales)[:, unstriped(offs)]
    y = unpack_fp4(w1_words, w1_scales).T @ xq
    z = f64(gn) * (d * (y[np.arange(H)[:, None], runs(n1, H)] - y) + 0.5 * ((d[np.arange(H)[:, None], runs(n3, H)]) * (y[np.arange(H)[:, None], runs(n2, H)] - y)))
    h = unpack_fp4(w3_words, w3_scales).T @ mxq(z, 0, "e4m3")
    sm = np.maximum(h, h[np.arange(N)[:, None], runs(n5, N)])
    ds = np.zeros((N, S))
    ds[np.arange(N)[:, None], runs(n4, N)] = sm
    out_0 = ds * sigmoid(h)
    return (out_0,) + planes(out_0)

@@ -1,0 +1,254 @@
+from contextlib import ExitStack
+
+import concourse.mybir as mybir
+
+K, T, S, N, H = 512, 2048, 512, 512, 512
+FLOPS = 3 * 2 * 512 * 512 * 512
+
+F32 = mybir.dt.float32
+BF16 = mybir.dt.bfloat16
+I32 = mybir.dt.int32
+U32 = mybir.dt.uint32
+U16 = mybir.dt.uint16
+U8 = mybir.dt.uint8
+FP8X4 = mybir.dt.float8_e4m3fn_x4
+FP4X4 = mybir.dt.float4_e2m1fn_x4
+ALU = mybir.AluOpType
+ACT = mybir.ActivationFunctionType
+
+P = 128
+PACK = 4
+WIDE = 384
+HALF = S // 2
+PER_COL = 16
+
+
+def load_scale_rows(queue, tile, scales):
+    width = scales.shape[2] // 4
+    for q in range(4):
+        rows = scales[0, 4 * q : 4 * q + 4, :].bitcast(I32)
+        queue.dma_start(out=tile[32 * q : 32 * q + 32, :].bitcast(I32), in_=rows.unsqueeze(0).to_broadcast([8, 4, width]))
+
+
+def deal_words(nc, dealt, raw):
+    nc.vector.tensor_copy(
+        out=dealt[:].rearrange("p (t m b) -> p t m b", t=PACK, b=2),
+        in_=raw[:].rearrange("p (m t b) -> p t m b", t=PACK, b=2),
+    )
+
+
+def deal_scales(nc, dealt, raw):
+    nc.vector.tensor_copy(
+        out=dealt[:].rearrange("p (t m) -> p t m", t=PACK),
+        in_=raw[:].rearrange("p (m t) -> p t m", t=PACK),
+    )
+
+
+def entries(lst, cols):
+    return lst[:, cols.start // PER_COL : cols.stop // PER_COL]
+
+
+def tile_picked_twlflowbsendg_none_po_kernel(
+    tc, x_words, x_scales, w1_words, w1_scales, w2_words, w2_scales, gn, w3_words, w3_scales,
+    offs, two, n1, n2, n3, n4, n5, out_0, out_1, out_2,
+):
+    nc = tc.nc
+    with ExitStack() as ctx:
+        keep = ctx.enter_context(tc.tile_pool(name="keep", bufs=1))
+        ring = ctx.enter_context(tc.tile_pool(name="ring", bufs=2))
+        psum = ctx.enter_context(tc.psum_pool(name="psum", bufs=1))
+
+        def list_tile(name, src):
+            tile = keep.tile([P, S // PER_COL], U16, name=name)
+            nc.sync.dma_start(tile[:], src)
+            return tile
+
+        def words_tile(name, src):
+            tile = keep.tile([P, 2 * H], U8, name=name)
+            nc.sync.dma_start(out=tile[:].bitcast(I32), in_=src[0].bitcast(I32))
+            return tile
+
+        def scales_tile(name, src):
+            tile = keep.tile([P, src.shape[2]], U8, name=name)
+            load_scale_rows(nc.sync, tile, src)
+            return tile
+
+        xw = keep.tile([P, T], I32, name="xw")
+        nc.scalar.dma_start(out=xw[:], in_=x_words[0].rearrange("p c r -> p (c r)").bitcast(I32))
+        l_offs = list_tile("l_offs", offs)
+        xs = scales_tile("xs", x_scales)
+        w1w = words_tile("w1w", w1_words)
+        l_two = list_tile("l_two", two)
+        w1s = scales_tile("w1s", w1_scales)
+        w2w = words_tile("w2w", w2_words)
+        l_n2 = list_tile("l_n2", n2)
+        l_n1 = list_tile("l_n1", n1)
+        w2s = scales_tile("w2s", w2_scales)
+        gain = keep.tile([P, PACK], F32, name="gain")
+        nc.sync.dma_start(out=gain[:], in_=gn.rearrange("(p t) o -> p (t o)", t=PACK))
+        l_n3 = list_tile("l_n3", n3)
+        w3w = words_tile("w3w", w3_words)
+        w3s = scales_tile("w3s", w3_scales)
+        l_n5 = list_tile("l_n5", n5)
+        l_n4 = list_tile("l_n4", n4)
+
+        def mx_tiles(name, width, word_dtype):
+            words = keep.tile([P, width], word_dtype, name=name + "_words", align_bytes=64)
+            scales = keep.tile([P, S], U8, name=name + "_scales", align_bytes=64)
+            return words, scales
+
+        xq_w, xq_s = mx_tiles("xq", S, U32)
+        xt_w, xt_s = mx_tiles("xt", S, U32)
+        d1_w, d1_s = mx_tiles("d1", 2 * H, U8)
+        d2_w, d2_s = mx_tiles("d2", 2 * H, U8)
+        d3_w, d3_s = mx_tiles("d3", 2 * H, U8)
+
+        nc.vector.tensor_copy(xq_s[:], xs[:].indirect(l_offs[:]))
+        deal_words(nc, d1_w, w1w)
+        nc.vector.tensor_copy(xq_w[:], xw[:].bitcast(U32).indirect(l_offs[:]))
+        deal_scales(nc, d1_s, w1s)
+        nc.vector.tensor_copy(xt_s[:], xs[:].indirect(l_two[:]))
+        nc.vector.tensor_copy(xt_w[:], xw[:].bitcast(U32).indirect(l_two[:]))
+        deal_words(nc, d2_w, w2w)
+        deal_scales(nc, d2_s, w2s)
+
+        def product(bank, w_words, w_scales, t, codes, scales, cols):
+            nc.tensor.matmul_mx(
+                out=bank[:, cols],
+                lhsT=w_words[:, 2 * P * t : 2 * P * (t + 1)].bitcast(FP4X4),
+                lhsT_scale=w_scales[:, P * t : P * (t + 1)],
+                rhs=codes[:, cols].bitcast(FP8X4),
+                rhs_scale=scales[:, cols],
+                start=True,
+                stop=True,
+            )
+
+        every = slice(0, S)
+        y_narrow, y_wide, dg = [], [], []
+        for t in range(PACK):
+            y_bank = psum.tile([P, S], F32, name="y_bank", tag="yh%d" % t)
+            product(y_bank, d1_w, d1_s, t, xq_w, xq_s, every)
+            d_bank = psum.tile([P, S], F32, name="d_bank", tag="d%d" % t)
+            product(d_bank, d2_w, d2_s, t, xt_w, xt_s, every)
+            y_wide.append(keep.tile([P, 2 * WIDE], F32, name="y_wide%d" % t))
+            y_narrow.append(keep.tile([P, S], F32, name="y_narrow%d" % t))
+            dg.append(keep.tile([P, S], F32, name="dg%d" % t))
+            nc.scalar.copy(y_wide[t][:, every], y_bank[:])
+            nc.scalar.copy(y_narrow[t][:], y_bank[:])
+            nc.scalar.activation(dg[t][:], d_bank[:], ACT.Copy, scale=gain[:, t : t + 1])
+
+        def z_tile(t, cols, window, plain, z_out, first_tile):
+            width = cols.stop - cols.start
+            diff1 = ring.tile([P, width], F32, name="diff1")
+            far = ring.tile([P, width], F32, name="far")
+            near = ring.tile([P, width], F32, name="near")
+            nc.vector.tensor_tensor(first_tile[:], window[:].indirect(entries(l_n2, cols)), plain[:, cols], ALU.subtract)
+            nc.vector.tensor_tensor(diff1[:], window[:].indirect(entries(l_n1, cols)), plain[:, cols], ALU.subtract)
+            nc.vector.tensor_tensor(far[:], dg[t][:].indirect(entries(l_n3, cols)), first_tile[:], ALU.mult)
+            nc.vector.tensor_tensor(near[:], dg[t][:, cols], diff1[:], ALU.mult)
+            nc.vector.scalar_tensor_tensor(z_out, far[:], 0.5, near[:], ALU.mult, ALU.add)
+
+        zq_w, zq_s = mx_tiles("zq", S, U32)
+        head = slice(0, WIDE)
+        tail = slice(WIDE, S)
+        z_head = keep.tile([P, PACK, WIDE], F32, name="z_head")
+        z_tail = keep.tile([P, PACK, S - WIDE], F32, name="z_tail")
+        for t in range(PACK):
+            diff2 = ring.tile([P, WIDE], F32, name="diff2")
+            z_tile(t, head, y_wide[t], y_narrow[t], z_head[:, t, :], diff2)
+        deal_words(nc, d3_w, w3w)
+        deal_scales(nc, d3_s, w3s)
+
+        zb_head = keep.tile([P, WIDE, PACK], BF16, name="zb_head", tag="held", align_bytes=64)
+        nc.scalar.copy(
+            zb_head[:].rearrange("p (c i) t -> p c t i", i=4),
+            z_head[:].rearrange("p t (c i) -> p c t i", i=4),
+        )
+        pieces = [slice(0, 256), slice(256, WIDE)]
+        for t in range(2):
+            diff2 = ring.tile([P, S - WIDE], F32, name="diff2")
+            z_tile(t, tail, y_narrow[t], y_wide[t], z_tail[:, t, :], diff2)
+        for cols in pieces:
+            nc.vector.quantize_mx(
+                out=zq_w[:, cols].bitcast(FP8X4), scales=zq_s[:, cols],
+                in_=zb_head[:, cols, :].rearrange("p c t -> p (c t)"),
+            )
+        h_bank, h_win, h_plain = [], [], []
+        for t in range(PACK):
+            h_bank.append(psum.tile([P, S], F32, name="h_bank", tag="yh%d" % t))
+            h_win.append(keep.tile([P, S], F32, name="h_win%d" % t))
+            h_plain.append(keep.tile([P, S], F32, name="h_plain%d" % t))
+            for cols in pieces:
+                product(h_bank[t], d3_w, d3_s, t, zq_w, zq_s, cols)
+            nc.scalar.copy(h_win[t][:, head], h_bank[t][:, head])
+            nc.scalar.copy(h_plain[t][:, head], h_bank[t][:, head])
+        diff2 = keep.tile([P, S - WIDE], F32, name="diff2_held", tag="held", align_bytes=64)
+        z_tile(2, tail, y_narrow[2], y_wide[2], z_tail[:, 2, :], diff2)
+        diff2 = ring.tile([P, S - WIDE], F32, name="diff2")
+        z_tile(3, tail, y_narrow[3], y_wide[3], z_tail[:, 3, :], diff2)
+
+        zb_tail = keep.tile([P, S - WIDE, PACK], BF16, name="zb_tail", align_bytes=64)
+        nc.vector.tensor_copy(
+            zb_tail[:].rearrange("p (c i) t -> p c t i", i=4),
+            z_tail[:].rearrange("p t (c i) -> p c t i", i=4),
+        )
+        nc.vector.quantize_mx(
+            out=zq_w[:, tail].bitcast(FP8X4), scales=zq_s[:, tail],
+            in_=zb_tail[:].rearrange("p c t -> p (c t)"),
+        )
+        for t in range(PACK):
+            product(h_bank[t], d3_w, d3_s, t, zq_w, zq_s, tail)
+            nc.scalar.copy(h_win[t][:, tail], h_bank[t][:, tail])
+            nc.scalar.copy(h_plain[t][:, tail], h_bank[t][:, tail])
+
+        halves = [slice(0, HALF), slice(HALF, S)]
+        excess, gate = [], []
+        for t in range(PACK):
+            gap = keep.tile([P, S], F32, name="gap%d" % t)
+            for cols in halves:
+                nc.vector.tensor_tensor(gap[:, cols], h_win[t][:].indirect(entries(l_n5, cols)), h_plain[t][:, cols], ALU.subtract)
+            excess.append(keep.tile([P, S], F32, name="excess%d" % t))
+            nc.scalar.activation(excess[t][:], gap[:], ACT.Relu)
+        for t in range(PACK):
+            gate.append(keep.tile([P, S], F32, name="gate%d" % t))
+            nc.scalar.activation(gate[t][:], h_bank[t][:], ACT.Sigmoid)
+
+        rows = out_0.rearrange("(p t) c -> p t c", t=PACK)
+        res = [keep.tile([P, 2, S], F32, name="res%d" % u) for u in range(2)]
+        ob = keep.tile([P, S, PACK], BF16, name="ob", align_bytes=64)
+        oq_w, oq_s = mx_tiles("oq", S, U32)
+        sent = []
+
+        def send(t, tag):
+            sent.append(keep.tile([P, 2 * S], F32, name="sent%d" % t, tag=tag))
+            nc.vector.tensor_tensor(sent[t][:].indirect(l_n4[:]), excess[t][:], h_plain[t][:], ALU.add)
+
+        def finish(t, cols):
+            nc.vector.tensor_tensor(res[t // 2][:, t % 2, cols], sent[t][:, cols], gate[t][:, cols], ALU.mult)
+            nc.sync.dma_start(out=rows[:, t, cols], in_=res[t // 2][:, t % 2, cols])
+
+        def pair_views(u, cols):
+            return ob[:, cols, 2 * u : 2 * u + 2], res[u][:, :, cols].rearrange("p e c -> p c e")
+
+        send(0, "sent0")
+        send(1, "sent1")
+        finish(0, every)
+        send(2, "sent2")
+        finish(1, every)
+        nc.scalar.copy(*pair_views(0, every))
+        finish(2, every)
+        send(3, "sent2")
+        for cols in halves:
+            finish(3, cols)
+        nc.scalar.copy(*pair_views(1, halves[0]))
+        nc.vector.tensor_copy(*pair_views(1, halves[1]))
+        words_out = out_1[0].rearrange("p c r -> p (c r)").bitcast(I32)
+        for cols in reversed(halves):
+            nc.vector.quantize_mx(
+                out=oq_w[:, cols].bitcast(FP8X4), scales=oq_s[:, cols],
+                in_=ob[:, cols, :].rearrange("p c t -> p (c t)"),
+            )
+            nc.sync.dma_start(out=words_out[:, cols], in_=oq_w[:, cols].bitcast(I32))
+        for q in range(4):
+            queue = nc.scalar if q % 2 == 0 else nc.sync
+            queue.dma_start(out=out_2[0, 4 * q : 4 * q + 4, :].bitcast(I32), in_=oq_s[32 * q : 32 * q + 4, :].bitcast(I32))

@@ -30,15 +30,15 @@ def load_scale_rows(queue, tile, scales):
         queue.dma_start(out=tile[32 * q : 32 * q + 32, :].bitcast(I32), in_=rows.unsqueeze(0).to_broadcast([8, 4, width]))
 
 
-def deal_words(nc, dealt, raw):
-    nc.vector.tensor_copy(
+def deal_words(engine, dealt, raw):
+    engine.tensor_copy(
         out=dealt[:].rearrange("p (t m b) -> p t m b", t=PACK, b=2),
         in_=raw[:].rearrange("p (m t b) -> p t m b", t=PACK, b=2),
     )
 
 
-def deal_scales(nc, dealt, raw):
-    nc.vector.tensor_copy(
+def deal_scales(engine, dealt, raw):
+    engine.tensor_copy(
         out=dealt[:].rearrange("p (t m) -> p t m", t=PACK),
         in_=raw[:].rearrange("p (m t) -> p t m", t=PACK),
     )
@@ -68,27 +68,27 @@ def tile_picked_twlflowbsendg_none_po_kernel(
             nc.sync.dma_start(out=tile[:].bitcast(I32), in_=src[0].bitcast(I32))
             return tile
 
-        def scales_tile(name, src):
-            tile = keep.tile([P, src.shape[2]], U8, name=name)
-            load_scale_rows(nc.sync, tile, src)
+        def scales_tile(name, src, queue):
+            tile = keep.tile([P, src.shape[2]], U8, name=name, align_bytes=64)
+            load_scale_rows(queue, tile, src)
             return tile
 
         xw = keep.tile([P, T], I32, name="xw")
-        nc.scalar.dma_start(out=xw[:], in_=x_words[0].rearrange("p c r -> p (c r)").bitcast(I32))
         l_offs = list_tile("l_offs", offs)
-        xs = scales_tile("xs", x_scales)
-        w1w = words_tile("w1w", w1_words)
+        xs = scales_tile("xs", x_scales, nc.sync)
         l_two = list_tile("l_two", two)
-        w1s = scales_tile("w1s", w1_scales)
+        w1w = words_tile("w1w", w1_words)
+        nc.sync.dma_start(out=xw[:], in_=x_words[0].rearrange("p c r -> p (c r)").bitcast(I32))
+        w1s = scales_tile("w1s", w1_scales, nc.sync)
         w2w = words_tile("w2w", w2_words)
+        w2s = scales_tile("w2s", w2_scales, nc.sync)
         l_n2 = list_tile("l_n2", n2)
         l_n1 = list_tile("l_n1", n1)
-        w2s = scales_tile("w2s", w2_scales)
         gain = keep.tile([P, PACK], F32, name="gain")
         nc.sync.dma_start(out=gain[:], in_=gn.rearrange("(p t) o -> p (t o)", t=PACK))
         l_n3 = list_tile("l_n3", n3)
         w3w = words_tile("w3w", w3_words)
-        w3s = scales_tile("w3s", w3_scales)
+        w3s = scales_tile("w3s", w3_scales, nc.sync)
         l_n5 = list_tile("l_n5", n5)
         l_n4 = list_tile("l_n4", n4)
 
@@ -98,19 +98,22 @@ def tile_picked_twlflowbsendg_none_po_kernel(
             return words, scales
 
         xq_w, xq_s = mx_tiles("xq", S, U32)
-        xt_w, xt_s = mx_tiles("xt", S, U32)
+        xt_s = keep.tile([P, S], U8, name="xt_scales", align_bytes=64)
         d1_w, d1_s = mx_tiles("d1", 2 * H, U8)
         d2_w, d2_s = mx_tiles("d2", 2 * H, U8)
         d3_w, d3_s = mx_tiles("d3", 2 * H, U8)
 
         nc.vector.tensor_copy(xq_s[:], xs[:].indirect(l_offs[:]))
-        deal_words(nc, d1_w, w1w)
-        nc.vector.tensor_copy(xq_w[:], xw[:].bitcast(U32).indirect(l_offs[:]))
-        deal_scales(nc, d1_s, w1s)
         nc.vector.tensor_copy(xt_s[:], xs[:].indirect(l_two[:]))
+        deal_words(nc.vector, d1_w, w1w)
+        nc.vector.tensor_copy(xq_w[:], xw[:].bitcast(U32).indirect(l_offs[:]))
+        deal_scales(nc.vector, d1_s, w1s)
+        xt_w = keep.tile([P, S], U32, name="xt_words", tag="w1s", align_bytes=64)
         nc.vector.tensor_copy(xt_w[:], xw[:].bitcast(U32).indirect(l_two[:]))
-        deal_words(nc, d2_w, w2w)
-        deal_scales(nc, d2_s, w2s)
+        deal_words(nc.vector, d2_w, w2w)
+        deal_scales(nc.vector, d2_s, w2s)
+        deal_words(nc.vector, d3_w, w3w)
+        deal_scales(nc.vector, d3_s, w3s)
 
         def product(bank, w_words, w_scales, t, codes, scales, cols):
             nc.tensor.matmul_mx(
@@ -137,17 +140,20 @@ def tile_picked_twlflowbsendg_none_po_kernel(
             nc.scalar.copy(y_narrow[t][:], y_bank[:])
             nc.scalar.activation(dg[t][:], d_bank[:], ACT.Copy, scale=gain[:, t : t + 1])
 
-        def z_tile(t, cols, window, plain, z_out, first_tile):
+        def z_terms(t, cols, window, plain, diff2):
             width = cols.stop - cols.start
             diff1 = ring.tile([P, width], F32, name="diff1")
             far = ring.tile([P, width], F32, name="far")
             near = ring.tile([P, width], F32, name="near")
-            nc.vector.tensor_tensor(first_tile[:], window[:].indirect(entries(l_n2, cols)), plain[:, cols], ALU.subtract)
+            nc.vector.tensor_tensor(diff2[:], window[:].indirect(entries(l_n2, cols)), plain[:, cols], ALU.subtract)
+            if pending:
+                nc.vector.scalar_tensor_tensor(*pending.pop(), ALU.mult, ALU.add)
             nc.vector.tensor_tensor(diff1[:], window[:].indirect(entries(l_n1, cols)), plain[:, cols], ALU.subtract)
-            nc.vector.tensor_tensor(far[:], dg[t][:].indirect(entries(l_n3, cols)), first_tile[:], ALU.mult)
+            nc.vector.tensor_tensor(far[:], dg[t][:].indirect(entries(l_n3, cols)), diff2[:], ALU.mult)
             nc.vector.tensor_tensor(near[:], dg[t][:, cols], diff1[:], ALU.mult)
-            nc.vector.scalar_tensor_tensor(z_out, far[:], 0.5, near[:], ALU.mult, ALU.add)
+            return far[:], 0.5, near[:]
 
+        pending = []
         zq_w, zq_s = mx_tiles("zq", S, U32)
         head = slice(0, WIDE)
         tail = slice(WIDE, S)
@@ -155,9 +161,9 @@ def tile_picked_twlflowbsendg_none_po_kernel(
         z_tail = keep.tile([P, PACK, S - WIDE], F32, name="z_tail")
         for t in range(PACK):
             diff2 = ring.tile([P, WIDE], F32, name="diff2")
-            z_tile(t, head, y_wide[t], y_narrow[t], z_head[:, t, :], diff2)
-        deal_words(nc, d3_w, w3w)
-        deal_scales(nc, d3_s, w3s)
+            pending.append((z_head[:, t, :], *z_terms(t, head, y_wide[t], y_narrow[t], diff2)))
+        diff2 = ring.tile([P, S - WIDE], F32, name="diff2")
+        pending.append((z_tail[:, 0, :], *z_terms(0, tail, y_narrow[0], y_wide[0], diff2)))
 
         zb_head = keep.tile([P, WIDE, PACK], BF16, name="zb_head", tag="held", align_bytes=64)
         nc.scalar.copy(
@@ -165,27 +171,25 @@ def tile_picked_twlflowbsendg_none_po_kernel(
             z_head[:].rearrange("p t (c i) -> p c t i", i=4),
         )
         pieces = [slice(0, 256), slice(256, WIDE)]
-        for t in range(2):
-            diff2 = ring.tile([P, S - WIDE], F32, name="diff2")
-            z_tile(t, tail, y_narrow[t], y_wide[t], z_tail[:, t, :], diff2)
+        diff2 = ring.tile([P, S - WIDE], F32, name="diff2")
+        pending.append((z_tail[:, 1, :], *z_terms(1, tail, y_narrow[1], y_wide[1], diff2)))
         for cols in pieces:
             nc.vector.quantize_mx(
                 out=zq_w[:, cols].bitcast(FP8X4), scales=zq_s[:, cols],
                 in_=zb_head[:, cols, :].rearrange("p c t -> p (c t)"),
             )
-        h_bank, h_win, h_plain = [], [], []
+        h_bank, h_win = [], []
         for t in range(PACK):
             h_bank.append(psum.tile([P, S], F32, name="h_bank", tag="yh%d" % t))
-            h_win.append(keep.tile([P, S], F32, name="h_win%d" % t))
-            h_plain.append(keep.tile([P, S], F32, name="h_plain%d" % t))
+            h_win.append(keep.tile([P, 2 * S], F32, name="h_win%d" % t))
             for cols in pieces:
                 product(h_bank[t], d3_w, d3_s, t, zq_w, zq_s, cols)
             nc.scalar.copy(h_win[t][:, head], h_bank[t][:, head])
-            nc.scalar.copy(h_plain[t][:, head], h_bank[t][:, head])
         diff2 = keep.tile([P, S - WIDE], F32, name="diff2_held", tag="held", align_bytes=64)
-        z_tile(2, tail, y_narrow[2], y_wide[2], z_tail[:, 2, :], diff2)
+        pending.append((z_tail[:, 2, :], *z_terms(2, tail, y_narrow[2], y_wide[2], diff2)))
         diff2 = ring.tile([P, S - WIDE], F32, name="diff2")
-        z_tile(3, tail, y_narrow[3], y_wide[3], z_tail[:, 3, :], diff2)
+        pending.append((z_tail[:, 3, :], *z_terms(3, tail, y_narrow[3], y_wide[3], diff2)))
+        nc.vector.scalar_tensor_tensor(*pending.pop(), ALU.mult, ALU.add)
 
         zb_tail = keep.tile([P, S - WIDE, PACK], BF16, name="zb_tail", align_bytes=64)
         nc.vector.tensor_copy(
@@ -199,16 +203,28 @@ def tile_picked_twlflowbsendg_none_po_kernel(
         for t in range(PACK):
             product(h_bank[t], d3_w, d3_s, t, zq_w, zq_s, tail)
             nc.scalar.copy(h_win[t][:, tail], h_bank[t][:, tail])
-            nc.scalar.copy(h_plain[t][:, tail], h_bank[t][:, tail])
 
         halves = [slice(0, HALF), slice(HALF, S)]
-        excess, gate = [], []
+        other, excess, larger, gate = [], [], [], []
         for t in range(PACK):
-            gap = keep.tile([P, S], F32, name="gap%d" % t)
-            for cols in halves:
-                nc.vector.tensor_tensor(gap[:, cols], h_win[t][:].indirect(entries(l_n5, cols)), h_plain[t][:, cols], ALU.subtract)
+            other.append(keep.tile([P, S], F32, name="other%d" % t))
+            nc.vector.tensor_copy(other[t][:], h_win[t][:].indirect(l_n5[:]))
+
+        def make_excess(t):
+            gap = ring.tile([P, S], F32, name="gap")
+            nc.gpsimd.tensor_tensor(gap[:], other[t][:], h_win[t][:, every], ALU.subtract)
             excess.append(keep.tile([P, S], F32, name="excess%d" % t))
             nc.scalar.activation(excess[t][:], gap[:], ACT.Relu)
+
+        def make_larger(t):
+            larger.append(keep.tile([P, S], F32, name="larger%d" % t))
+            nc.gpsimd.tensor_tensor(larger[t][:], excess[t][:], h_win[t][:, every], ALU.add)
+
+        for t0 in (0, 2):
+            make_excess(t0)
+            make_excess(t0 + 1)
+            make_larger(t0)
+            make_larger(t0 + 1)
         for t in range(PACK):
             gate.append(keep.tile([P, S], F32, name="gate%d" % t))
             nc.scalar.activation(gate[t][:], h_bank[t][:], ACT.Sigmoid)
@@ -219,27 +235,24 @@ def tile_picked_twlflowbsendg_none_po_kernel(
         oq_w, oq_s = mx_tiles("oq", S, U32)
         sent = []
 
-        def send(t, tag):
-            sent.append(keep.tile([P, 2 * S], F32, name="sent%d" % t, tag=tag))
-            nc.vector.tensor_tensor(sent[t][:].indirect(l_n4[:]), excess[t][:], h_plain[t][:], ALU.add)
+        def send(t):
+            sent.append(keep.tile([P, 2 * S], F32, name="sent%d" % t))
+            nc.vector.tensor_copy(sent[t][:].indirect(l_n4[:]), larger[t][:])
 
-        def finish(t, cols):
-            nc.vector.tensor_tensor(res[t // 2][:, t % 2, cols], sent[t][:, cols], gate[t][:, cols], ALU.mult)
+        def finish(engine, t, cols):
+            engine.tensor_tensor(res[t // 2][:, t % 2, cols], sent[t][:, cols], gate[t][:, cols], ALU.mult)
             nc.sync.dma_start(out=rows[:, t, cols], in_=res[t // 2][:, t % 2, cols])
 
         def pair_views(u, cols):
             return ob[:, cols, 2 * u : 2 * u + 2], res[u][:, :, cols].rearrange("p e c -> p c e")
 
-        send(0, "sent0")
-        send(1, "sent1")
-        finish(0, every)
-        send(2, "sent2")
-        finish(1, every)
+        for t in range(PACK - 1):
+            send(t)
+            finish(nc.gpsimd, t, every)
         nc.scalar.copy(*pair_views(0, every))
-        finish(2, every)
-        send(3, "sent2")
+        send(3)
         for cols in halves:
-            finish(3, cols)
+            finish(nc.vector, 3, cols)
         nc.scalar.copy(*pair_views(1, halves[0]))
         nc.vector.tensor_copy(*pair_views(1, halves[1]))
         words_out = out_1[0].rearrange("p c r -> p (c r)").bitcast(I32)

@@ -1,6 +1,7 @@
 from contextlib import ExitStack
 
 import concourse.mybir as mybir
+from concourse.masks import make_identity
 
 K, T, S, N, H = 512, 2048, 512, 512, 512
 FLOPS = 3 * 2 * 512 * 512 * 512
@@ -21,6 +22,7 @@ PACK = 4
 WIDE = 384
 HALF = S // 2
 PER_COL = 16
+FUSED = 2
 
 
 def load_scale_rows(queue, tile, scales):
@@ -55,7 +57,7 @@ def tile_picked_twlflowbsendg_none_po_kernel(
     nc = tc.nc
     with ExitStack() as ctx:
         keep = ctx.enter_context(tc.tile_pool(name="keep", bufs=1))
-        ring = ctx.enter_context(tc.tile_pool(name="ring", bufs=2))
+        ring = ctx.enter_context(tc.tile_pool(name="ring", bufs=3))
         psum = ctx.enter_context(tc.psum_pool(name="psum", bufs=1))
 
         def list_tile(name, src):
@@ -81,13 +83,13 @@ def tile_picked_twlflowbsendg_none_po_kernel(
         nc.sync.dma_start(out=xw[:], in_=x_words[0].rearrange("p c r -> p (c r)").bitcast(I32))
         w1s = scales_tile("w1s", w1_scales, nc.sync)
         w2w = words_tile("w2w", w2_words)
+        w3w = words_tile("w3w", w3_words)
         w2s = scales_tile("w2s", w2_scales, nc.sync)
         l_n2 = list_tile("l_n2", n2)
         l_n1 = list_tile("l_n1", n1)
         gain = keep.tile([P, PACK], F32, name="gain")
         nc.sync.dma_start(out=gain[:], in_=gn.rearrange("(p t) o -> p (t o)", t=PACK))
         l_n3 = list_tile("l_n3", n3)
-        w3w = words_tile("w3w", w3_words)
         w3s = scales_tile("w3s", w3_scales, nc.sync)
         l_n5 = list_tile("l_n5", n5)
         l_n4 = list_tile("l_n4", n4)
@@ -105,14 +107,20 @@ def tile_picked_twlflowbsendg_none_po_kernel(
 
         nc.vector.tensor_copy(xq_s[:], xs[:].indirect(l_offs[:]))
         nc.vector.tensor_copy(xt_s[:], xs[:].indirect(l_two[:]))
-        deal_words(nc.vector, d1_w, w1w)
-        nc.vector.tensor_copy(xq_w[:], xw[:].bitcast(U32).indirect(l_offs[:]))
         deal_scales(nc.vector, d1_s, w1s)
+        halves = [slice(0, HALF), slice(HALF, S)]
+        for cols in halves:
+            nc.vector.tensor_copy(xq_w[:, cols], xw[:].bitcast(U32).indirect(entries(l_offs, cols)))
         xt_w = keep.tile([P, S], U32, name="xt_words", tag="w1s", align_bytes=64)
         nc.vector.tensor_copy(xt_w[:], xw[:].bitcast(U32).indirect(l_two[:]))
-        deal_words(nc.vector, d2_w, w2w)
-        deal_scales(nc.vector, d2_s, w2s)
-        deal_words(nc.vector, d3_w, w3w)
+        ident = keep.tile([P, P], F32, name="ident")
+        make_identity(nc, ident[:])
+        warm = keep.tile([P, 1], F32, name="warm")
+        nc.scalar.activation(warm[:], ident[:, 0:1], ACT.Sigmoid)
+        deal_words(nc.gpsimd, d1_w, w1w)
+        deal_words(nc.gpsimd, d2_w, w2w)
+        deal_scales(nc.gpsimd, d2_s, w2s)
+        deal_words(nc.gpsimd, d3_w, w3w)
         deal_scales(nc.vector, d3_s, w3s)
 
         def product(bank, w_words, w_scales, t, codes, scales, cols):
@@ -129,15 +137,17 @@ def tile_picked_twlflowbsendg_none_po_kernel(
         every = slice(0, S)
         y_narrow, y_wide, dg = [], [], []
         for t in range(PACK):
-            y_bank = psum.tile([P, S], F32, name="y_bank", tag="yh%d" % t)
-            product(y_bank, d1_w, d1_s, t, xq_w, xq_s, every)
-            d_bank = psum.tile([P, S], F32, name="d_bank", tag="d%d" % t)
-            product(d_bank, d2_w, d2_s, t, xt_w, xt_s, every)
             y_wide.append(keep.tile([P, 2 * WIDE], F32, name="y_wide%d" % t))
             y_narrow.append(keep.tile([P, S], F32, name="y_narrow%d" % t))
             dg.append(keep.tile([P, S], F32, name="dg%d" % t))
-            nc.scalar.copy(y_wide[t][:, every], y_bank[:])
-            nc.scalar.copy(y_narrow[t][:], y_bank[:])
+            parts = zip(halves, ("yh0", "d3")) if t == 0 else [(every, "yh%d" % t)]
+            for cols, bank_tag in parts:
+                y_bank = psum.tile([P, S], F32, name="y_bank", tag=bank_tag)
+                product(y_bank, d1_w, d1_s, t, xq_w, xq_s, cols)
+                nc.scalar.copy(y_wide[t][:, cols], y_bank[:, cols])
+                nc.scalar.copy(y_narrow[t][:, cols], y_bank[:, cols])
+            d_bank = psum.tile([P, S], F32, name="d_bank", tag="d%d" % t)
+            product(d_bank, d2_w, d2_s, t, xt_w, xt_s, every)
             nc.scalar.activation(dg[t][:], d_bank[:], ACT.Copy, scale=gain[:, t : t + 1])
 
         def z_terms(t, cols, window, plain, diff2):
@@ -147,90 +157,103 @@ def tile_picked_twlflowbsendg_none_po_kernel(
             near = ring.tile([P, width], F32, name="near")
             nc.vector.tensor_tensor(diff2[:], window[:].indirect(entries(l_n2, cols)), plain[:, cols], ALU.subtract)
             if pending:
-                nc.vector.scalar_tensor_tensor(*pending.pop(), ALU.mult, ALU.add)
+                nc.vector.tensor_tensor(*pending.pop(), ALU.add)
             nc.vector.tensor_tensor(diff1[:], window[:].indirect(entries(l_n1, cols)), plain[:, cols], ALU.subtract)
             nc.vector.tensor_tensor(far[:], dg[t][:].indirect(entries(l_n3, cols)), diff2[:], ALU.mult)
-            nc.vector.tensor_tensor(near[:], dg[t][:, cols], diff1[:], ALU.mult)
-            return far[:], 0.5, near[:]
+            nc.vector.scalar_tensor_tensor(near[:], dg[t][:, cols], 2.0, diff1[:], ALU.mult, ALU.mult)
+            return far, near
 
         pending = []
         zq_w, zq_s = mx_tiles("zq", S, U32)
         head = slice(0, WIDE)
         tail = slice(WIDE, S)
-        z_head = keep.tile([P, PACK, WIDE], F32, name="z_head")
+        blocks = WIDE // P
+        z_turned = [psum.tile([P, PACK, P], F32, name="z_turned", tag="d%d" % b) for b in range(blocks)]
         z_tail = keep.tile([P, PACK, S - WIDE], F32, name="z_tail")
         for t in range(PACK):
             diff2 = ring.tile([P, WIDE], F32, name="diff2")
-            pending.append((z_head[:, t, :], *z_terms(t, head, y_wide[t], y_narrow[t], diff2)))
-        diff2 = ring.tile([P, S - WIDE], F32, name="diff2")
-        pending.append((z_tail[:, 0, :], *z_terms(0, tail, y_narrow[0], y_wide[0], diff2)))
+            far, near = z_terms(t, head, y_wide[t], y_narrow[t], diff2)
+            for b in range(blocks):
+                for term in (far, near):
+                    nc.tensor.matmul(
+                        z_turned[b][:, t, :], lhsT=term[:, P * b : P * (b + 1)], rhs=ident[:],
+                        start=term is far, stop=term is near, is_transpose=True,
+                    )
 
         zb_head = keep.tile([P, WIDE, PACK], BF16, name="zb_head", tag="held", align_bytes=64)
-        nc.scalar.copy(
-            zb_head[:].rearrange("p (c i) t -> p c t i", i=4),
-            z_head[:].rearrange("p t (c i) -> p c t i", i=4),
-        )
+        zb_words = zb_head[:].rearrange("p c t -> p (c t)").bitcast(F32).rearrange("p (c u) -> p c u", u=2)
+        for b in range(blocks):
+            pairs = ring.tile([P, 2, P, 2], BF16, name="pairs")
+            nc.scalar.activation(pairs[:], z_turned[b][:].rearrange("j (u e) p -> j u p e", e=2), ACT.Copy, scale=0.5)
+            back = psum.tile([P, 2, P], F32, name="back", tag="d%d" % b)
+            for u in range(2):
+                nc.tensor.transpose(back[:, u, :], pairs[:, u, :, :].rearrange("j p e -> j (p e)").bitcast(F32), ident[:])
+            nc.scalar.copy(zb_words[:, P * b : P * (b + 1), :], back[:].rearrange("p u c -> p c u"))
+
+        def tail_terms(t, diff2):
+            far, near = z_terms(t, tail, y_narrow[t], y_wide[t], diff2)
+            pending.append((z_tail[:, t, :], far[:], near[:]))
+
+        for t in range(PACK - 1):
+            tail_terms(t, ring.tile([P, S - WIDE], F32, name="diff2"))
         pieces = [slice(0, 256), slice(256, WIDE)]
-        diff2 = ring.tile([P, S - WIDE], F32, name="diff2")
-        pending.append((z_tail[:, 1, :], *z_terms(1, tail, y_narrow[1], y_wide[1], diff2)))
         for cols in pieces:
             nc.vector.quantize_mx(
                 out=zq_w[:, cols].bitcast(FP8X4), scales=zq_s[:, cols],
                 in_=zb_head[:, cols, :].rearrange("p c t -> p (c t)"),
             )
-        h_bank, h_win = [], []
+        h_bank, h_win, h_plain = [], [], []
         for t in range(PACK):
             h_bank.append(psum.tile([P, S], F32, name="h_bank", tag="yh%d" % t))
             h_win.append(keep.tile([P, 2 * S], F32, name="h_win%d" % t))
-            for cols in pieces:
-                product(h_bank[t], d3_w, d3_s, t, zq_w, zq_s, cols)
-            nc.scalar.copy(h_win[t][:, head], h_bank[t][:, head])
-        diff2 = keep.tile([P, S - WIDE], F32, name="diff2_held", tag="held", align_bytes=64)
-        pending.append((z_tail[:, 2, :], *z_terms(2, tail, y_narrow[2], y_wide[2], diff2)))
-        diff2 = ring.tile([P, S - WIDE], F32, name="diff2")
-        pending.append((z_tail[:, 3, :], *z_terms(3, tail, y_narrow[3], y_wide[3], diff2)))
-        nc.vector.scalar_tensor_tensor(*pending.pop(), ALU.mult, ALU.add)
+            if t < FUSED:
+                h_plain.append(keep.tile([P, S], F32, name="h_plain%d" % t))
+                for cols in pieces:
+                    product(h_bank[t], d3_w, d3_s, t, zq_w, zq_s, cols)
+                nc.scalar.copy(h_win[t][:, head], h_bank[t][:, head])
+                nc.scalar.copy(h_plain[t][:, head], h_bank[t][:, head])
+        tail_terms(3, keep.tile([P, S - WIDE], F32, name="diff2_held", tag="held", align_bytes=64))
+        nc.vector.tensor_tensor(*pending.pop(), ALU.add)
 
         zb_tail = keep.tile([P, S - WIDE, PACK], BF16, name="zb_tail", align_bytes=64)
-        nc.vector.tensor_copy(
+        nc.vector.tensor_scalar(
             zb_tail[:].rearrange("p (c i) t -> p c t i", i=4),
             z_tail[:].rearrange("p t (c i) -> p c t i", i=4),
+            0.5, None, ALU.mult,
         )
         nc.vector.quantize_mx(
             out=zq_w[:, tail].bitcast(FP8X4), scales=zq_s[:, tail],
             in_=zb_tail[:].rearrange("p c t -> p (c t)"),
         )
         for t in range(PACK):
-            product(h_bank[t], d3_w, d3_s, t, zq_w, zq_s, tail)
-            nc.scalar.copy(h_win[t][:, tail], h_bank[t][:, tail])
+            cols = tail if t < FUSED else every
+            product(h_bank[t], d3_w, d3_s, t, zq_w, zq_s, cols)
+            nc.scalar.copy(h_win[t][:, cols], h_bank[t][:, cols])
+            if t < FUSED:
+                nc.scalar.copy(h_plain[t][:, tail], h_bank[t][:, tail])
 
-        halves = [slice(0, HALF), slice(HALF, S)]
-        other, excess, larger, gate = [], [], [], []
+        gap, excess, larger, gate = [], [], [], []
         for t in range(PACK):
-            other.append(keep.tile([P, S], F32, name="other%d" % t))
-            nc.vector.tensor_copy(other[t][:], h_win[t][:].indirect(l_n5[:]))
-
-        def make_excess(t):
-            gap = ring.tile([P, S], F32, name="gap")
-            nc.gpsimd.tensor_tensor(gap[:], other[t][:], h_win[t][:, every], ALU.subtract)
-            excess.append(keep.tile([P, S], F32, name="excess%d" % t))
-            nc.scalar.activation(excess[t][:], gap[:], ACT.Relu)
-
-        def make_larger(t):
+            if t < FUSED:
+                gap.append(keep.tile([P, S], F32, name="gap%d" % t))
             larger.append(keep.tile([P, S], F32, name="larger%d" % t))
-            nc.gpsimd.tensor_tensor(larger[t][:], excess[t][:], h_win[t][:, every], ALU.add)
-
-        for t0 in (0, 2):
-            make_excess(t0)
-            make_excess(t0 + 1)
-            make_larger(t0)
-            make_larger(t0 + 1)
+        for cols in halves:
+            nc.vector.tensor_tensor(gap[0][:, cols], h_win[0][:].indirect(entries(l_n5, cols)), h_plain[0][:, cols], ALU.subtract)
+        nc.vector.tensor_tensor(gap[1][:], h_win[1][:].indirect(l_n5[:]), h_plain[1][:], ALU.subtract)
         for t in range(PACK):
-            gate.append(keep.tile([P, S], F32, name="gate%d" % t))
+            if t >= FUSED:
+                other = keep.tile([P, S], F32, name="other%d" % t)
+                nc.vector.tensor_copy(other[:], h_win[t][:].indirect(l_n5[:]))
+                gap.append(keep.tile([P, S], F32, name="gap", tag="excess%d" % (t - 1)))
+                nc.gpsimd.tensor_tensor(gap[t][:], other[:], h_win[t][:, every], ALU.subtract)
+            excess.append(keep.tile([P, S], F32, name="excess%d" % t))
+            nc.scalar.activation(excess[t][:], gap[t][:], ACT.Relu)
+            nc.gpsimd.tensor_tensor(larger[t][:], excess[t][:], h_win[t][:, every], ALU.add)
+            gate.append(keep.tile([P, S], F32, name="gate", tag="gap%d" % t if t < FUSED else "excess%d" % (t - 1)))
             nc.scalar.activation(gate[t][:], h_bank[t][:], ACT.Sigmoid)
 
         rows = out_0.rearrange("(p t) c -> p t c", t=PACK)
-        res = [keep.tile([P, 2, S], F32, name="res%d" % u) for u in range(2)]
+        res = [keep.tile([P, 2, S], F32, name="res", tag="h_win%d" % (2 + u)) for u in range(2)]
         ob = keep.tile([P, S, PACK], BF16, name="ob", align_bytes=64)
         oq_w, oq_s = mx_tiles("oq", S, U32)
         sent = []
@@ -251,17 +274,22 @@ def tile_picked_twlflowbsendg_none_po_kernel(
             finish(nc.gpsimd, t, every)
         nc.scalar.copy(*pair_views(0, every))
         send(3)
+        quarters = [slice(HALF, WIDE), slice(WIDE, S)]
+        for cols in [halves[0]] + quarters:
+            nc.vector.tensor_tensor(res[1][:, 1, cols], sent[3][:, cols], gate[3][:, cols], ALU.mult)
         for cols in halves:
-            finish(nc.vector, 3, cols)
+            nc.sync.dma_start(out=rows[:, 3, cols], in_=res[1][:, 1, cols])
         nc.scalar.copy(*pair_views(1, halves[0]))
-        nc.vector.tensor_copy(*pair_views(1, halves[1]))
-        words_out = out_1[0].rearrange("p c r -> p (c r)").bitcast(I32)
-        for cols in reversed(halves):
+        for cols in quarters:
+            nc.vector.tensor_copy(*pair_views(1, cols))
+        for cols in quarters + [halves[0]]:
             nc.vector.quantize_mx(
                 out=oq_w[:, cols].bitcast(FP8X4), scales=oq_s[:, cols],
                 in_=ob[:, cols, :].rearrange("p c t -> p (c t)"),
             )
+        words_out = out_1[0].rearrange("p c r -> p (c r)").bitcast(I32)
+        for cols in reversed(halves):
             nc.sync.dma_start(out=words_out[:, cols], in_=oq_w[:, cols].bitcast(I32))
         for q in range(4):
-            queue = nc.scalar if q % 2 == 0 else nc.sync
+            queue = nc.scalar if q < 3 else nc.sync
             queue.dma_start(out=out_2[0, 4 * q : 4 * q + 4, :].bitcast(I32), in_=oq_s[32 * q : 32 * q + 4, :].bitcast(I32))

@@ -32,17 +32,17 @@ def load_scale_rows(queue, tile, scales):
         queue.dma_start(out=tile[32 * q : 32 * q + 32, :].bitcast(I32), in_=rows.unsqueeze(0).to_broadcast([8, 4, width]))
 
 
-def deal_words(engine, dealt, raw):
+def deal_words(engine, dealt, raw, slots):
     engine.tensor_copy(
-        out=dealt[:].rearrange("p (t m b) -> p t m b", t=PACK, b=2),
-        in_=raw[:].rearrange("p (m t b) -> p t m b", t=PACK, b=2),
+        out=dealt[:].rearrange("p (t m b) -> p t m b", m=P, b=2),
+        in_=raw[:].rearrange("p (m t b) -> p t m b", t=PACK, b=2)[:, slots],
     )
 
 
-def deal_scales(engine, dealt, raw):
+def deal_scales(engine, dealt, raw, slots):
     engine.tensor_copy(
-        out=dealt[:].rearrange("p (t m) -> p t m", t=PACK),
-        in_=raw[:].rearrange("p (m t) -> p t m", t=PACK),
+        out=dealt[:].rearrange("p (t m) -> p t m", m=P),
+        in_=raw[:].rearrange("p (m t) -> p t m", t=PACK)[:, slots],
     )
 
 
@@ -65,9 +65,9 @@ def tile_picked_twlflowbsendg_none_po_kernel(
             nc.sync.dma_start(tile[:], src)
             return tile
 
-        def words_tile(name, src):
+        def words_tile(name, src, queue):
             tile = keep.tile([P, 2 * H], U8, name=name)
-            nc.sync.dma_start(out=tile[:].bitcast(I32), in_=src[0].bitcast(I32))
+            queue.dma_start(out=tile[:].bitcast(I32), in_=src[0].bitcast(I32))
             return tile
 
         def scales_tile(name, src, queue):
@@ -79,18 +79,18 @@ def tile_picked_twlflowbsendg_none_po_kernel(
         l_offs = list_tile("l_offs", offs)
         xs = scales_tile("xs", x_scales, nc.sync)
         l_two = list_tile("l_two", two)
-        w1w = words_tile("w1w", w1_words)
+        w1w = words_tile("w1w", w1_words, nc.sync)
         nc.sync.dma_start(out=xw[:], in_=x_words[0].rearrange("p c r -> p (c r)").bitcast(I32))
         w1s = scales_tile("w1s", w1_scales, nc.sync)
-        w2w = words_tile("w2w", w2_words)
-        w3w = words_tile("w3w", w3_words)
+        w2w = words_tile("w2w", w2_words, nc.gpsimd)
+        w3w = words_tile("w3w", w3_words, nc.gpsimd)
         w2s = scales_tile("w2s", w2_scales, nc.sync)
-        l_n2 = list_tile("l_n2", n2)
         l_n1 = list_tile("l_n1", n1)
+        l_n2 = list_tile("l_n2", n2)
         gain = keep.tile([P, PACK], F32, name="gain")
         nc.sync.dma_start(out=gain[:], in_=gn.rearrange("(p t) o -> p (t o)", t=PACK))
-        l_n3 = list_tile("l_n3", n3)
         w3s = scales_tile("w3s", w3_scales, nc.sync)
+        l_n3 = list_tile("l_n3", n3)
         l_n5 = list_tile("l_n5", n5)
         l_n4 = list_tile("l_n4", n4)
 
@@ -103,11 +103,14 @@ def tile_picked_twlflowbsendg_none_po_kernel(
         xt_s = keep.tile([P, S], U8, name="xt_scales", align_bytes=64)
         d1_w, d1_s = mx_tiles("d1", 2 * H, U8)
         d2_w, d2_s = mx_tiles("d2", 2 * H, U8)
-        d3_w, d3_s = mx_tiles("d3", 2 * H, U8)
+        d3a_w = keep.tile([P, 2 * P * FUSED], U8, name="d3a_words", align_bytes=64)
+        d3a_s = keep.tile([P, P * FUSED], U8, name="d3a_scales", align_bytes=64)
+        all_slots, early, late = slice(0, PACK), slice(0, FUSED), slice(FUSED, PACK)
 
         nc.vector.tensor_copy(xq_s[:], xs[:].indirect(l_offs[:]))
         nc.vector.tensor_copy(xt_s[:], xs[:].indirect(l_two[:]))
-        deal_scales(nc.vector, d1_s, w1s)
+        deal_words(nc.vector, d1_w, w1w, all_slots)
+        deal_scales(nc.vector, d1_s, w1s, all_slots)
         halves = [slice(0, HALF), slice(HALF, S)]
         for cols in halves:
             nc.vector.tensor_copy(xq_w[:, cols], xw[:].bitcast(U32).indirect(entries(l_offs, cols)))
@@ -117,11 +120,10 @@ def tile_picked_twlflowbsendg_none_po_kernel(
         make_identity(nc, ident[:])
         warm = keep.tile([P, 1], F32, name="warm")
         nc.scalar.activation(warm[:], ident[:, 0:1], ACT.Sigmoid)
-        deal_words(nc.gpsimd, d1_w, w1w)
-        deal_words(nc.gpsimd, d2_w, w2w)
-        deal_scales(nc.gpsimd, d2_s, w2s)
-        deal_words(nc.gpsimd, d3_w, w3w)
-        deal_scales(nc.vector, d3_s, w3s)
+        deal_words(nc.gpsimd, d2_w, w2w, all_slots)
+        deal_words(nc.gpsimd, d3a_w, w3w, early)
+        deal_scales(nc.gpsimd, d2_s, w2s, all_slots)
+        deal_scales(nc.gpsimd, d3a_s, w3s, early)
 
         def product(bank, w_words, w_scales, t, codes, scales, cols):
             nc.tensor.matmul_mx(
@@ -150,52 +152,54 @@ def tile_picked_twlflowbsendg_none_po_kernel(
             product(d_bank, d2_w, d2_s, t, xt_w, xt_s, every)
             nc.scalar.activation(dg[t][:], d_bank[:], ACT.Copy, scale=gain[:, t : t + 1])
 
-        def z_terms(t, cols, window, plain, diff2):
+        def z_terms(t, cols, window, plain, near_factor, diff1):
             width = cols.stop - cols.start
-            diff1 = ring.tile([P, width], F32, name="diff1")
+            diff2 = ring.tile([P, width], F32, name="diff2")
             far = ring.tile([P, width], F32, name="far")
             near = ring.tile([P, width], F32, name="near")
-            nc.vector.tensor_tensor(diff2[:], window[:].indirect(entries(l_n2, cols)), plain[:, cols], ALU.subtract)
-            if pending:
-                nc.vector.tensor_tensor(*pending.pop(), ALU.add)
             nc.vector.tensor_tensor(diff1[:], window[:].indirect(entries(l_n1, cols)), plain[:, cols], ALU.subtract)
+            nc.vector.tensor_tensor(diff2[:], window[:].indirect(entries(l_n2, cols)), plain[:, cols], ALU.subtract)
+            nc.vector.scalar_tensor_tensor(near[:], dg[t][:, cols], near_factor, diff1[:], ALU.mult, ALU.mult)
             nc.vector.tensor_tensor(far[:], dg[t][:].indirect(entries(l_n3, cols)), diff2[:], ALU.mult)
-            nc.vector.scalar_tensor_tensor(near[:], dg[t][:, cols], 2.0, diff1[:], ALU.mult, ALU.mult)
-            return far, near
+            return near, far
 
-        pending = []
+        def add_turned(banks, t, terms):
+            for i, term in enumerate(terms):
+                for b, bank in enumerate(banks):
+                    nc.tensor.matmul(
+                        bank[:, t, :], lhsT=term[:, P * b : P * (b + 1)], rhs=ident[:],
+                        start=i == 0, stop=i == 1, is_transpose=True,
+                    )
+
+        def turn_back(turned, bank_tag, n_pairs, out_words):
+            pairs = ring.tile([P, n_pairs, P, 2], BF16, name="pairs")
+            nc.scalar.activation(pairs[:], turned[:].rearrange("j (u e) p -> j u p e", e=2), ACT.Copy, scale=0.5)
+            back = psum.tile([P, n_pairs, P], F32, name="back", tag=bank_tag)
+            for u in range(n_pairs):
+                nc.tensor.transpose(back[:, u, :], pairs[:, u, :, :].rearrange("j p e -> j (p e)").bitcast(F32), ident[:])
+            nc.scalar.copy(out_words, back[:].rearrange("p u c -> p c u"))
+
+        def as_words(tile):
+            return tile[:].rearrange("p c t -> p (c t)").bitcast(F32).rearrange("p (c u) -> p c u", u=2)
+
         zq_w, zq_s = mx_tiles("zq", S, U32)
         head = slice(0, WIDE)
         tail = slice(WIDE, S)
         blocks = WIDE // P
-        z_turned = [psum.tile([P, PACK, P], F32, name="z_turned", tag="d%d" % b) for b in range(blocks)]
-        z_tail = keep.tile([P, PACK, S - WIDE], F32, name="z_tail")
+        turned = [psum.tile([P, PACK, P], F32, name="turned", tag="d%d" % b) for b in range(blocks)]
         for t in range(PACK):
-            diff2 = ring.tile([P, WIDE], F32, name="diff2")
-            far, near = z_terms(t, head, y_wide[t], y_narrow[t], diff2)
-            for b in range(blocks):
-                for term in (far, near):
-                    nc.tensor.matmul(
-                        z_turned[b][:, t, :], lhsT=term[:, P * b : P * (b + 1)], rhs=ident[:],
-                        start=term is far, stop=term is near, is_transpose=True,
-                    )
-
+            diff1 = ring.tile([P, WIDE], F32, name="diff1")
+            add_turned(turned, t, z_terms(t, head, y_wide[t], y_narrow[t], 2.0, diff1))
         zb_head = keep.tile([P, WIDE, PACK], BF16, name="zb_head", tag="held", align_bytes=64)
-        zb_words = zb_head[:].rearrange("p c t -> p (c t)").bitcast(F32).rearrange("p (c u) -> p c u", u=2)
         for b in range(blocks):
-            pairs = ring.tile([P, 2, P, 2], BF16, name="pairs")
-            nc.scalar.activation(pairs[:], z_turned[b][:].rearrange("j (u e) p -> j u p e", e=2), ACT.Copy, scale=0.5)
-            back = psum.tile([P, 2, P], F32, name="back", tag="d%d" % b)
-            for u in range(2):
-                nc.tensor.transpose(back[:, u, :], pairs[:, u, :, :].rearrange("j p e -> j (p e)").bitcast(F32), ident[:])
-            nc.scalar.copy(zb_words[:, P * b : P * (b + 1), :], back[:].rearrange("p u c -> p c u"))
+            turn_back(turned[b], "d%d" % b, 2, as_words(zb_head)[:, P * b : P * (b + 1), :])
 
-        def tail_terms(t, diff2):
-            far, near = z_terms(t, tail, y_narrow[t], y_wide[t], diff2)
-            pending.append((z_tail[:, t, :], far[:], near[:]))
-
-        for t in range(PACK - 1):
-            tail_terms(t, ring.tile([P, S - WIDE], F32, name="diff2"))
+        zb_tail = keep.tile([P, S - WIDE, PACK], BF16, name="zb_tail", align_bytes=64)
+        turned_tail = psum.tile([P, 2, P], F32, name="turned_tail", tag="d3")
+        for t in range(2):
+            diff1 = ring.tile([P, S - WIDE], F32, name="diff1")
+            add_turned([turned_tail], t, z_terms(t, tail, y_narrow[t], y_wide[t], 2.0, diff1))
+        turn_back(turned_tail, "d3", 1, as_words(zb_tail)[:, :, 0:1])
         pieces = [slice(0, 256), slice(256, WIDE)]
         for cols in pieces:
             nc.vector.quantize_mx(
@@ -209,28 +213,29 @@ def tile_picked_twlflowbsendg_none_po_kernel(
             if t < FUSED:
                 h_plain.append(keep.tile([P, S], F32, name="h_plain%d" % t))
                 for cols in pieces:
-                    product(h_bank[t], d3_w, d3_s, t, zq_w, zq_s, cols)
+                    product(h_bank[t], d3a_w, d3a_s, t, zq_w, zq_s, cols)
                 nc.scalar.copy(h_win[t][:, head], h_bank[t][:, head])
                 nc.scalar.copy(h_plain[t][:, head], h_bank[t][:, head])
-        tail_terms(3, keep.tile([P, S - WIDE], F32, name="diff2_held", tag="held", align_bytes=64))
-        nc.vector.tensor_tensor(*pending.pop(), ALU.add)
-
-        zb_tail = keep.tile([P, S - WIDE, PACK], BF16, name="zb_tail", align_bytes=64)
-        nc.vector.tensor_scalar(
-            zb_tail[:].rearrange("p (c i) t -> p c t i", i=4),
-            z_tail[:].rearrange("p t (c i) -> p c t i", i=4),
-            0.5, None, ALU.mult,
-        )
+        diff1 = ring.tile([P, S - WIDE], F32, name="diff1")
+        diff1_held = keep.tile([P, S - WIDE], F32, name="diff1_held", tag="held", align_bytes=64)
+        terms = [z_terms(t, tail, y_narrow[t], y_wide[t], 1.0, first) for t, first in ((2, diff1), (3, diff1_held))]
+        for t, (near, far) in zip((2, 3), terms):
+            nc.vector.scalar_tensor_tensor(zb_tail[:, :, t], far[:], 0.5, near[:], ALU.mult, ALU.add)
         nc.vector.quantize_mx(
             out=zq_w[:, tail].bitcast(FP8X4), scales=zq_s[:, tail],
             in_=zb_tail[:].rearrange("p c t -> p (c t)"),
         )
-        for t in range(PACK):
-            cols = tail if t < FUSED else every
-            product(h_bank[t], d3_w, d3_s, t, zq_w, zq_s, cols)
-            nc.scalar.copy(h_win[t][:, cols], h_bank[t][:, cols])
-            if t < FUSED:
-                nc.scalar.copy(h_plain[t][:, tail], h_bank[t][:, tail])
+        for t in range(FUSED):
+            product(h_bank[t], d3a_w, d3a_s, t, zq_w, zq_s, tail)
+            nc.scalar.copy(h_win[t][:, tail], h_bank[t][:, tail])
+            nc.scalar.copy(h_plain[t][:, tail], h_bank[t][:, tail])
+        d3b = keep.tile([P, 3 * P * (PACK - FUSED)], U8, name="d3b", tag="zb_tail", align_bytes=64)
+        d3b_w, d3b_s = d3b[:, : 2 * P * (PACK - FUSED)], d3b[:, 2 * P * (PACK - FUSED) :]
+        deal_words(nc.vector, d3b_w, w3w, late)
+        deal_scales(nc.vector, d3b_s, w3s, late)
+        for t in range(FUSED, PACK):
+            product(h_bank[t], d3b_w, d3b_s, t - FUSED, zq_w, zq_s, every)
+            nc.scalar.copy(h_win[t][:, every], h_bank[t][:])
 
         gap, excess, larger, gate = [], [], [], []
         for t in range(PACK):
@@ -240,20 +245,21 @@ def tile_picked_twlflowbsendg_none_po_kernel(
         for cols in halves:
             nc.vector.tensor_tensor(gap[0][:, cols], h_win[0][:].indirect(entries(l_n5, cols)), h_plain[0][:, cols], ALU.subtract)
         nc.vector.tensor_tensor(gap[1][:], h_win[1][:].indirect(l_n5[:]), h_plain[1][:], ALU.subtract)
+        h_rows = h_plain + h_win[FUSED:]
         for t in range(PACK):
             if t >= FUSED:
                 other = keep.tile([P, S], F32, name="other%d" % t)
                 nc.vector.tensor_copy(other[:], h_win[t][:].indirect(l_n5[:]))
                 gap.append(keep.tile([P, S], F32, name="gap", tag="excess%d" % (t - 1)))
-                nc.gpsimd.tensor_tensor(gap[t][:], other[:], h_win[t][:, every], ALU.subtract)
+                nc.gpsimd.tensor_tensor(gap[t][:], other[:], h_rows[t][:, every], ALU.subtract)
             excess.append(keep.tile([P, S], F32, name="excess%d" % t))
             nc.scalar.activation(excess[t][:], gap[t][:], ACT.Relu)
-            nc.gpsimd.tensor_tensor(larger[t][:], excess[t][:], h_win[t][:, every], ALU.add)
+            nc.gpsimd.tensor_tensor(larger[t][:], excess[t][:], h_rows[t][:, every], ALU.add)
             gate.append(keep.tile([P, S], F32, name="gate", tag="gap%d" % t if t < FUSED else "excess%d" % (t - 1)))
             nc.scalar.activation(gate[t][:], h_bank[t][:], ACT.Sigmoid)
 
         rows = out_0.rearrange("(p t) c -> p t c", t=PACK)
-        res = [keep.tile([P, 2, S], F32, name="res", tag="h_win%d" % (2 + u)) for u in range(2)]
+        res = [keep.tile([P, 2, S], F32, name="res", tag=slot) for slot in ("h_win2", "h_win3")]
         ob = keep.tile([P, S, PACK], BF16, name="ob", align_bytes=64)
         oq_w, oq_s = mx_tiles("oq", S, U32)
         sent = []

from contextlib import ExitStack

import concourse.mybir as mybir
from concourse.masks import make_identity

K, T, S, N, H = 512, 2048, 512, 512, 512
FLOPS = 3 * 2 * 512 * 512 * 512

F32 = mybir.dt.float32
BF16 = mybir.dt.bfloat16
I32 = mybir.dt.int32
U32 = mybir.dt.uint32
U16 = mybir.dt.uint16
U8 = mybir.dt.uint8
FP8X4 = mybir.dt.float8_e4m3fn_x4
FP4X4 = mybir.dt.float4_e2m1fn_x4
ALU = mybir.AluOpType
ACT = mybir.ActivationFunctionType

P = 128
PACK = 4
WIDE = 384
HALF = S // 2
PER_COL = 16
FUSED = 2


def load_scale_rows(queue, tile, scales):
    width = scales.shape[2] // 4
    for q in range(4):
        rows = scales[0, 4 * q : 4 * q + 4, :].bitcast(I32)
        queue.dma_start(out=tile[32 * q : 32 * q + 32, :].bitcast(I32), in_=rows.unsqueeze(0).to_broadcast([8, 4, width]))


def deal_words(engine, dealt, raw, slots):
    engine.tensor_copy(
        out=dealt[:].rearrange("p (t m b) -> p t m b", m=P, b=2),
        in_=raw[:].rearrange("p (m t b) -> p t m b", t=PACK, b=2)[:, slots],
    )


def deal_scales(engine, dealt, raw, slots):
    engine.tensor_copy(
        out=dealt[:].rearrange("p (t m) -> p t m", m=P),
        in_=raw[:].rearrange("p (m t) -> p t m", t=PACK)[:, slots],
    )


def entries(lst, cols):
    return lst[:, cols.start // PER_COL : cols.stop // PER_COL]


def tile_picked_twlflowbsendg_none_po_kernel(
    tc, x_words, x_scales, w1_words, w1_scales, w2_words, w2_scales, gn, w3_words, w3_scales,
    offs, two, n1, n2, n3, n4, n5, out_0, out_1, out_2,
):
    nc = tc.nc
    with ExitStack() as ctx:
        keep = ctx.enter_context(tc.tile_pool(name="keep", bufs=1))
        ring = ctx.enter_context(tc.tile_pool(name="ring", bufs=3))
        psum = ctx.enter_context(tc.psum_pool(name="psum", bufs=1))

        def list_tile(name, src):
            tile = keep.tile([P, S // PER_COL], U16, name=name)
            nc.sync.dma_start(tile[:], src)
            return tile

        def words_tile(name, src, queue):
            tile = keep.tile([P, 2 * H], U8, name=name)
            queue.dma_start(out=tile[:].bitcast(I32), in_=src[0].bitcast(I32))
            return tile

        def scales_tile(name, src, queue):
            tile = keep.tile([P, src.shape[2]], U8, name=name, align_bytes=64)
            load_scale_rows(queue, tile, src)
            return tile

        xw = keep.tile([P, T], I32, name="xw")
        l_offs = list_tile("l_offs", offs)
        xs = scales_tile("xs", x_scales, nc.sync)
        l_two = list_tile("l_two", two)
        w1w = words_tile("w1w", w1_words, nc.sync)
        nc.sync.dma_start(out=xw[:], in_=x_words[0].rearrange("p c r -> p (c r)").bitcast(I32))
        w1s = scales_tile("w1s", w1_scales, nc.sync)
        w2w = words_tile("w2w", w2_words, nc.gpsimd)
        w3w = words_tile("w3w", w3_words, nc.gpsimd)
        w2s = scales_tile("w2s", w2_scales, nc.sync)
        l_n1 = list_tile("l_n1", n1)
        l_n2 = list_tile("l_n2", n2)
        gain = keep.tile([P, PACK], F32, name="gain")
        nc.sync.dma_start(out=gain[:], in_=gn.rearrange("(p t) o -> p (t o)", t=PACK))
        w3s = scales_tile("w3s", w3_scales, nc.sync)
        l_n3 = list_tile("l_n3", n3)
        l_n5 = list_tile("l_n5", n5)
        l_n4 = list_tile("l_n4", n4)

        def mx_tiles(name, width, word_dtype):
            words = keep.tile([P, width], word_dtype, name=name + "_words", align_bytes=64)
            scales = keep.tile([P, S], U8, name=name + "_scales", align_bytes=64)
            return words, scales

        xq_w, xq_s = mx_tiles("xq", S, U32)
        xt_s = keep.tile([P, S], U8, name="xt_scales", align_bytes=64)
        d1_w, d1_s = mx_tiles("d1", 2 * H, U8)
        d2_w, d2_s = mx_tiles("d2", 2 * H, U8)
        d3a_w = keep.tile([P, 2 * P * FUSED], U8, name="d3a_words", align_bytes=64)
        d3a_s = keep.tile([P, P * FUSED], U8, name="d3a_scales", align_bytes=64)
        all_slots, early, late = slice(0, PACK), slice(0, FUSED), slice(FUSED, PACK)

        nc.vector.tensor_copy(xq_s[:], xs[:].indirect(l_offs[:]))
        nc.vector.tensor_copy(xt_s[:], xs[:].indirect(l_two[:]))
        deal_words(nc.vector, d1_w, w1w, all_slots)
        deal_scales(nc.vector, d1_s, w1s, all_slots)
        halves = [slice(0, HALF), slice(HALF, S)]
        for cols in halves:
            nc.vector.tensor_copy(xq_w[:, cols], xw[:].bitcast(U32).indirect(entries(l_offs, cols)))
        xt_w = keep.tile([P, S], U32, name="xt_words", tag="w1s", align_bytes=64)
        nc.vector.tensor_copy(xt_w[:], xw[:].bitcast(U32).indirect(l_two[:]))
        ident = keep.tile([P, P], F32, name="ident")
        make_identity(nc, ident[:])
        warm = keep.tile([P, 1], F32, name="warm")
        nc.scalar.activation(warm[:], ident[:, 0:1], ACT.Sigmoid)
        deal_words(nc.gpsimd, d2_w, w2w, all_slots)
        deal_words(nc.gpsimd, d3a_w, w3w, early)
        deal_scales(nc.gpsimd, d2_s, w2s, all_slots)
        deal_scales(nc.gpsimd, d3a_s, w3s, early)

        def product(bank, w_words, w_scales, t, codes, scales, cols):
            nc.tensor.matmul_mx(
                out=bank[:, cols],
                lhsT=w_words[:, 2 * P * t : 2 * P * (t + 1)].bitcast(FP4X4),
                lhsT_scale=w_scales[:, P * t : P * (t + 1)],
                rhs=codes[:, cols].bitcast(FP8X4),
                rhs_scale=scales[:, cols],
                start=True,
                stop=True,
            )

        every = slice(0, S)
        y_narrow, y_wide, dg = [], [], []
        for t in range(PACK):
            y_wide.append(keep.tile([P, 2 * WIDE], F32, name="y_wide%d" % t))
            y_narrow.append(keep.tile([P, S], F32, name="y_narrow%d" % t))
            dg.append(keep.tile([P, S], F32, name="dg%d" % t))
            parts = zip(halves, ("yh0", "d3")) if t == 0 else [(every, "yh%d" % t)]
            for cols, bank_tag in parts:
                y_bank = psum.tile([P, S], F32, name="y_bank", tag=bank_tag)
                product(y_bank, d1_w, d1_s, t, xq_w, xq_s, cols)
                nc.scalar.copy(y_wide[t][:, cols], y_bank[:, cols])
                nc.scalar.copy(y_narrow[t][:, cols], y_bank[:, cols])
            d_bank = psum.tile([P, S], F32, name="d_bank", tag="d%d" % t)
            product(d_bank, d2_w, d2_s, t, xt_w, xt_s, every)
            nc.scalar.activation(dg[t][:], d_bank[:], ACT.Copy, scale=gain[:, t : t + 1])

        def z_terms(t, cols, window, plain, near_factor, diff1):
            width = cols.stop - cols.start
            diff2 = ring.tile([P, width], F32, name="diff2")
            far = ring.tile([P, width], F32, name="far")
            near = ring.tile([P, width], F32, name="near")
            nc.vector.tensor_tensor(diff1[:], window[:].indirect(entries(l_n1, cols)), plain[:, cols], ALU.subtract)
            nc.vector.tensor_tensor(diff2[:], window[:].indirect(entries(l_n2, cols)), plain[:, cols], ALU.subtract)
            nc.vector.scalar_tensor_tensor(near[:], dg[t][:, cols], near_factor, diff1[:], ALU.mult, ALU.mult)
            nc.vector.tensor_tensor(far[:], dg[t][:].indirect(entries(l_n3, cols)), diff2[:], ALU.mult)
            return near, far

        def add_turned(banks, t, terms):
            for i, term in enumerate(terms):
                for b, bank in enumerate(banks):
                    nc.tensor.matmul(
                        bank[:, t, :], lhsT=term[:, P * b : P * (b + 1)], rhs=ident[:],
                        start=i == 0, stop=i == 1, is_transpose=True,
                    )

        def turn_back(turned, bank_tag, n_pairs, out_words):
            pairs = ring.tile([P, n_pairs, P, 2], BF16, name="pairs")
            nc.scalar.activation(pairs[:], turned[:].rearrange("j (u e) p -> j u p e", e=2), ACT.Copy, scale=0.5)
            back = psum.tile([P, n_pairs, P], F32, name="back", tag=bank_tag)
            for u in range(n_pairs):
                nc.tensor.transpose(back[:, u, :], pairs[:, u, :, :].rearrange("j p e -> j (p e)").bitcast(F32), ident[:])
            nc.scalar.copy(out_words, back[:].rearrange("p u c -> p c u"))

        def as_words(tile):
            return tile[:].rearrange("p c t -> p (c t)").bitcast(F32).rearrange("p (c u) -> p c u", u=2)

        zq_w, zq_s = mx_tiles("zq", S, U32)
        head = slice(0, WIDE)
        tail = slice(WIDE, S)
        blocks = WIDE // P
        turned = [psum.tile([P, PACK, P], F32, name="turned", tag="d%d" % b) for b in range(blocks)]
        for t in range(PACK):
            diff1 = ring.tile([P, WIDE], F32, name="diff1")
            add_turned(turned, t, z_terms(t, head, y_wide[t], y_narrow[t], 2.0, diff1))
        zb_head = keep.tile([P, WIDE, PACK], BF16, name="zb_head", tag="held", align_bytes=64)
        for b in range(blocks):
            turn_back(turned[b], "d%d" % b, 2, as_words(zb_head)[:, P * b : P * (b + 1), :])

        zb_tail = keep.tile([P, S - WIDE, PACK], BF16, name="zb_tail", align_bytes=64)
        turned_tail = psum.tile([P, 2, P], F32, name="turned_tail", tag="d3")
        for t in range(2):
            diff1 = ring.tile([P, S - WIDE], F32, name="diff1")
            add_turned([turned_tail], t, z_terms(t, tail, y_narrow[t], y_wide[t], 2.0, diff1))
        turn_back(turned_tail, "d3", 1, as_words(zb_tail)[:, :, 0:1])
        pieces = [slice(0, 256), slice(256, WIDE)]
        for cols in pieces:
            nc.vector.quantize_mx(
                out=zq_w[:, cols].bitcast(FP8X4), scales=zq_s[:, cols],
                in_=zb_head[:, cols, :].rearrange("p c t -> p (c t)"),
            )
        h_bank, h_win, h_plain = [], [], []
        for t in range(PACK):
            h_bank.append(psum.tile([P, S], F32, name="h_bank", tag="yh%d" % t))
            h_win.append(keep.tile([P, 2 * S], F32, name="h_win%d" % t))
            if t < FUSED:
                h_plain.append(keep.tile([P, S], F32, name="h_plain%d" % t))
                for cols in pieces:
                    product(h_bank[t], d3a_w, d3a_s, t, zq_w, zq_s, cols)
                nc.scalar.copy(h_win[t][:, head], h_bank[t][:, head])
                nc.scalar.copy(h_plain[t][:, head], h_bank[t][:, head])
        diff1 = ring.tile([P, S - WIDE], F32, name="diff1")
        diff1_held = keep.tile([P, S - WIDE], F32, name="diff1_held", tag="held", align_bytes=64)
        terms = [z_terms(t, tail, y_narrow[t], y_wide[t], 1.0, first) for t, first in ((2, diff1), (3, diff1_held))]
        for t, (near, far) in zip((2, 3), terms):
            nc.vector.scalar_tensor_tensor(zb_tail[:, :, t], far[:], 0.5, near[:], ALU.mult, ALU.add)
        nc.vector.quantize_mx(
            out=zq_w[:, tail].bitcast(FP8X4), scales=zq_s[:, tail],
            in_=zb_tail[:].rearrange("p c t -> p (c t)"),
        )
        for t in range(FUSED):
            product(h_bank[t], d3a_w, d3a_s, t, zq_w, zq_s, tail)
            nc.scalar.copy(h_win[t][:, tail], h_bank[t][:, tail])
            nc.scalar.copy(h_plain[t][:, tail], h_bank[t][:, tail])
        d3b = keep.tile([P, 3 * P * (PACK - FUSED)], U8, name="d3b", tag="zb_tail", align_bytes=64)
        d3b_w, d3b_s = d3b[:, : 2 * P * (PACK - FUSED)], d3b[:, 2 * P * (PACK - FUSED) :]
        deal_words(nc.vector, d3b_w, w3w, late)
        deal_scales(nc.vector, d3b_s, w3s, late)
        for t in range(FUSED, PACK):
            product(h_bank[t], d3b_w, d3b_s, t - FUSED, zq_w, zq_s, every)
            nc.scalar.copy(h_win[t][:, every], h_bank[t][:])

        gap, excess, larger, gate = [], [], [], []
        for t in range(PACK):
            if t < FUSED:
                gap.append(keep.tile([P, S], F32, name="gap%d" % t))
            larger.append(keep.tile([P, S], F32, name="larger%d" % t))
        for cols in halves:
            nc.vector.tensor_tensor(gap[0][:, cols], h_win[0][:].indirect(entries(l_n5, cols)), h_plain[0][:, cols], ALU.subtract)
        nc.vector.tensor_tensor(gap[1][:], h_win[1][:].indirect(l_n5[:]), h_plain[1][:], ALU.subtract)
        h_rows = h_plain + h_win[FUSED:]
        for t in range(PACK):
            if t >= FUSED:
                other = keep.tile([P, S], F32, name="other%d" % t)
                nc.vector.tensor_copy(other[:], h_win[t][:].indirect(l_n5[:]))
                gap.append(keep.tile([P, S], F32, name="gap", tag="excess%d" % (t - 1)))
                nc.gpsimd.tensor_tensor(gap[t][:], other[:], h_rows[t][:, every], ALU.subtract)
            excess.append(keep.tile([P, S], F32, name="excess%d" % t))
            nc.scalar.activation(excess[t][:], gap[t][:], ACT.Relu)
            nc.gpsimd.tensor_tensor(larger[t][:], excess[t][:], h_rows[t][:, every], ALU.add)
            gate.append(keep.tile([P, S], F32, name="gate", tag="gap%d" % t if t < FUSED else "excess%d" % (t - 1)))
            nc.scalar.activation(gate[t][:], h_bank[t][:], ACT.Sigmoid)

        rows = out_0.rearrange("(p t) c -> p t c", t=PACK)
        res = [keep.tile([P, 2, S], F32, name="res", tag=slot) for slot in ("h_win2", "h_win3")]
        ob = keep.tile([P, S, PACK], BF16, name="ob", align_bytes=64)
        oq_w, oq_s = mx_tiles("oq", S, U32)
        sent = []

        def send(t):
            sent.append(keep.tile([P, 2 * S], F32, name="sent%d" % t))
            nc.vector.tensor_copy(sent[t][:].indirect(l_n4[:]), larger[t][:])

        def finish(engine, t, cols):
            engine.tensor_tensor(res[t // 2][:, t % 2, cols], sent[t][:, cols], gate[t][:, cols], ALU.mult)
            nc.sync.dma_start(out=rows[:, t, cols], in_=res[t // 2][:, t % 2, cols])

        def pair_views(u, cols):
            return ob[:, cols, 2 * u : 2 * u + 2], res[u][:, :, cols].rearrange("p e c -> p c e")

        for t in range(PACK - 1):
            send(t)
            finish(nc.gpsimd, t, every)
        nc.scalar.copy(*pair_views(0, every))
        send(3)
        quarters = [slice(HALF, WIDE), slice(WIDE, S)]
        for cols in [halves[0]] + quarters:
            nc.vector.tensor_tensor(res[1][:, 1, cols], sent[3][:, cols], gate[3][:, cols], ALU.mult)
        for cols in halves:
            nc.sync.dma_start(out=rows[:, 3, cols], in_=res[1][:, 1, cols])
        nc.scalar.copy(*pair_views(1, halves[0]))
        for cols in quarters:
            nc.vector.tensor_copy(*pair_views(1, cols))
        for cols in quarters + [halves[0]]:
            nc.vector.quantize_mx(
                out=oq_w[:, cols].bitcast(FP8X4), scales=oq_s[:, cols],
                in_=ob[:, cols, :].rearrange("p c t -> p (c t)"),
            )
        words_out = out_1[0].rearrange("p c r -> p (c r)").bitcast(I32)
        for cols in reversed(halves):
            nc.sync.dma_start(out=words_out[:, cols], in_=oq_w[:, cols].bitcast(I32))
        for q in range(4):
            queue = nc.scalar if q < 3 else nc.sync
            queue.dma_start(out=out_2[0, 4 * q : 4 * q + 4, :].bitcast(I32), in_=oq_s[32 * q : 32 * q + 4, :].bitcast(I32))
